import numpy as np
import ml_dtypes


def mxq(x, axis, fmt="e4m3"):
    dtype, down = {"e4m3": (ml_dtypes.float8_e4m3fn, 7), "e5m2": (ml_dtypes.float8_e5m2, 14)}[fmt]
    v = np.moveaxis(np.asarray(x, np.float32).astype(ml_dtypes.bfloat16).astype(np.float64), axis, -1)
    blocks = v.reshape(v.shape[:-1] + (-1, 32))
    amax = np.abs(blocks).max(-1, keepdims=True)
    byte = np.maximum(np.where(amax > 0, np.frexp(amax)[1] - 1 + 127, 0) - down, 1)
    scale = np.exp2(byte - 127.0)
    codes = (blocks / scale).astype(np.float32).astype(dtype).astype(np.float64)
    return np.moveaxis((codes * scale).reshape(v.shape), -1, axis)


WIDE = False


def mx_kscale(k):
    if not WIDE:
        return np.ones(k)
    levels = np.array([10, -10, 5, -5, 0])
    if k % 512:
        return np.exp2(np.random.permutation(np.resize(levels, k // 32))).repeat(32)
    a = np.empty((k // 512, 16))
    for p in range(k // 512):
        a[p, :8] = np.random.permutation(np.resize(levels, 8))
        for g in range(8):
            far = levels[np.abs(levels - a[p, g]) >= 10]
            a[p, g + 8] = far[np.random.randint(len(far))]
    return np.exp2(a.ravel()).repeat(32)


def f64(x):
    return np.asarray(x).astype(np.float64)


def striped(idx):
    return np.tile(idx.reshape(-1, 16).T, (8, 1)).astype(np.uint16)


def unstriped(offs):
    return offs[:16].T.reshape(-1).astype(np.int64)


def striped8(idx):
    return np.concatenate([x.reshape(-1, 16).T for x in idx]).astype(np.uint16)


def runs(offs, k):
    lists = np.stack([offs[16 * r : 16 * r + 16].T.reshape(-1) for r in range(8)]).astype(np.int64)
    return lists[np.arange(k) % 512 // 64]


def pack_weight(w):
    k, n = w.shape
    w = f64(np.asarray(w, np.float32).astype(ml_dtypes.bfloat16)).reshape(k // 32, 32, n)
    amax = np.abs(w).max(1)
    byte = np.clip(np.where(amax > 0, np.frexp(amax)[1] - 1 + 127 - 7, 1), 1, 254)
    scaled = (w * np.exp2(127.0 - byte)[:, None, :]).reshape(k, n).astype(np.float32)
    words = np.ascontiguousarray(scaled.reshape(k // 512, 128, 4, n).transpose(0, 1, 3, 2)).astype(ml_dtypes.float8_e4m3fn).view(np.uint8)
    return words, np.ascontiguousarray(byte.astype(np.uint8).reshape(k // 512, 16, n))


def unpack_weight(words, scales):
    g, p, n, _ = words.shape
    vals = np.ascontiguousarray(words).view(ml_dtypes.float8_e4m3fn).astype(np.float64) * np.repeat(np.exp2(scales.astype(np.float64) - 127.0), 8, axis=1)[..., None]
    return vals.transpose(0, 1, 3, 2).reshape(g * 512, n)


def sigmoid(v):
    return 1.0 / (1.0 + np.exp(-np.maximum(v, -700.0)))

def planes(y):
    n, m = y.shape
    v = y.astype(np.float32).astype(ml_dtypes.bfloat16).astype(np.float64).reshape(n // 32, 32, m)
    top = np.abs(v).max(1)
    byte = np.clip(np.where(top > 0, np.frexp(top)[1] - 1 + 127 - 7, 1), 1, 254)
    codes = (v * np.exp2(127.0 - byte)[:, None, :]).reshape(n, m).astype(np.float32).astype(ml_dtypes.float8_e4m3fn).view(np.uint8)
    words = codes.reshape(n // 512, 128, 4, m).transpose(0, 1, 3, 2)
    return np.ascontiguousarray(words), np.ascontiguousarray(byte.astype(np.uint8).reshape(n // 512, 16, m))


K, T, S, H, C, G, W = 512, 1024, 512, 512, 512, 2048, 256


def setup_inputs():
    n = np.random.standard_normal
    s = mx_kscale(K)[:, None]
    packed_xT = pack_weight(n((K, T)) * s)
    packed_w1 = pack_weight(n((K, H)) / np.sqrt(K) / s)
    packed_dT = pack_weight(n((K, G)) / s)
    return {
        "x_words": packed_xT[0],
        "x_scales": packed_xT[1],
        "w1_words": packed_w1[0],
        "w1_scales": packed_w1[1],
        "gs": (np.random.uniform(0.5, 1.5, (K, 1)) / s).astype(np.float32),
        "gk": (np.random.uniform(0.5, 1.5, (K, 1)) * s).astype(np.float32),
        "d_words": packed_dT[0],
        "d_scales": packed_dT[1],
        "offs": striped(np.random.permutation(T)[:S]),
        "n1": striped8(np.stack([np.random.permutation(S) for _ in range(8)])),
        "n2": striped8(np.stack([np.random.permutation(S) for _ in range(8)])),
        "n3": striped(np.random.permutation(S)),
        "n4": striped(np.random.permutation(S)),
        "cand": striped(np.random.permutation(T)[:C]),
        "k1": striped8(np.random.randint(0, G, (8, H))),
        "n5": striped8(np.stack([np.random.permutation(S)[:W] for _ in range(8)])),
        "n6": striped8(np.stack([np.random.permutation(S)[:W] for _ in range(8)])),
    }


def reference(x_words, x_scales, w1_words, w1_scales, gs, gk, d_words, d_scales, offs, n1, n2, n3, n4, cand, k1, n5, n6):
    d_k1 = unpack_weight(d_words, d_scales)[np.arange(K)[:, None], runs(k1, K)]
    xq = unpack_weight(x_words, x_scales)[:, unstriped(offs)]
    y = unpack_weight(w1_words, w1_scales).T @ xq
    st = y - y[:, unstriped(n3)]
    z2 = f64(gk) * (st / (np.abs(st[:, unstriped(n4)]) + 0.5))
    b = 0.0625 * ((d_k1.T @ mxq(z2, 0, "e4m3")))
    x_cand = unpack_weight(x_words, x_scales)[:, unstriped(cand)]
    z = f64(gs) * (np.maximum(y * (sigmoid(y[np.arange(H)[:, None], runs(n1, H)])), y[np.arange(H)[:, None], runs(n2, H)]))
    a = 0.0625 * ((x_cand.T @ mxq(z, 0, "e4m3")))
    ra = b[np.arange(H)[:, None], runs(n6, H)] - (0.5 * (a[np.arange(C)[:, None], runs(n5, C)]))
    out = a.copy()
    out[np.arange(H)[:, None], runs(n5, H)] = ra
    return (out,) + planes(out)

@@ -1,0 +1,253 @@
+from contextlib import ExitStack
+
+import concourse.mybir as mybir
+
+F32 = mybir.dt.float32
+BF16 = mybir.dt.bfloat16
+I32 = mybir.dt.int32
+U32 = mybir.dt.uint32
+U16 = mybir.dt.uint16
+U8 = mybir.dt.uint8
+FP8X4 = mybir.dt.float8_e4m3fn_x4
+ALU = mybir.AluOpType
+ACT = mybir.ActivationFunctionType
+
+P = 128
+PACK = 4
+S = 512
+W = 256
+T = 1024
+G = 2048
+FLOPS = 3 * 2 * 512 * 512 * 512
+TINY = 2.0**-60
+
+
+def tile_picked_cdkeyputbgmaxhopn_none_po_kernel(
+    tc, x_words, x_scales, w1_words, w1_scales, gs, gk, d_words, d_scales, offs, n1, n2, n3, n4, cand, k1, n5, n6, out_0, out_1, out_2
+):
+    nc = tc.nc
+    planes = range(PACK)
+
+    def words_of(packed):
+        return packed[0].rearrange("p n r -> p (n r)").bitcast(I32)
+
+    with ExitStack() as ctx:
+        lists = ctx.enter_context(tc.tile_pool(name="lists", bufs=1))
+        sb = ctx.enter_context(tc.tile_pool(name="sb", bufs=1))
+        psum = ctx.enter_context(tc.psum_pool(name="psum", bufs=1))
+
+        def load_list(dram, name):
+            tile = lists.tile([P, dram.shape[1]], U16, name=name)
+            nc.sync.dma_start(tile[:], dram)
+            return tile
+
+        def zeroed_bytes(width, name):
+            tile = sb.tile([P, width], U8, name=name, align_bytes=64)
+            nc.vector.memset(tile[:].bitcast(I32), 0)
+            return tile
+
+        def load_scale_rows(queue, tile, dram):
+            for q in range(4):
+                queue.dma_start(tile[32 * q : 32 * q + 4, :].bitcast(I32), dram[0, 4 * q : 4 * q + 4, :].bitcast(I32))
+
+        def deal_words(src, name):
+            dealt = sb.tile([P, S], I32, name=name, align_bytes=64)
+            nc.vector.tensor_copy(
+                dealt[:].rearrange("p (t c i) -> p c t i", t=PACK, i=4),
+                src[:].rearrange("p (c i t) -> p c t i", t=PACK, i=4),
+            )
+            return dealt
+
+        def deal_bytes(src, name):
+            dealt = sb.tile([P, S], U8, name=name, align_bytes=64)
+            nc.vector.tensor_copy(
+                dealt[:].rearrange("p (t m) -> p t m", t=PACK),
+                src[:].rearrange("p (m t) -> p t m", t=PACK),
+            )
+            return dealt
+
+        def gather_words(table, offsets, name, tag=None):
+            picked = sb.tile([P, S], I32, name=name, tag=tag or name, align_bytes=64)
+            nc.vector.tensor_copy(picked[:].bitcast(U32), table[:].bitcast(U32).indirect(offsets[:]))
+            return picked
+
+        def gather_bytes(table, offsets, name, tag=None):
+            picked = sb.tile([P, S], U8, name=name, tag=tag or name, align_bytes=64)
+            nc.vector.tensor_copy(picked[:], table[:].indirect(offsets[:]))
+            return picked
+
+        def product(bank, t, lhs_words, lhs_scales, rhs_words, rhs_scales, first_row=0):
+            cols = slice(P * t, P * (t + 1))
+            nc.tensor.matmul_mx(
+                out=bank[:],
+                lhsT=lhs_words[:, cols].bitcast(FP8X4),
+                lhsT_scale=lhs_scales[first_row:, cols],
+                rhs=rhs_words[:].bitcast(FP8X4),
+                rhs_scale=rhs_scales[:],
+                start=True,
+                stop=True,
+            )
+
+        def weave(stacked, name, scalar_cols=0):
+            woven = sb.tile([P, S, PACK], BF16, name=name + "_woven", align_bytes=64)
+            split = S - scalar_cols
+            nc.vector.tensor_copy(
+                woven[:, :split, :].rearrange("p (c i) t -> p c t i", i=4),
+                stacked[:, :, :split].rearrange("p t (c i) -> p c t i", i=4),
+            )
+            if scalar_cols:
+                nc.scalar.copy(
+                    woven[:, split:, :].rearrange("p (c i) t -> p c t i", i=4),
+                    stacked[:, :, split:].rearrange("p t (c i) -> p c t i", i=4),
+                )
+            return woven
+
+        def quantise(woven, name):
+            codes = sb.tile([P, S], I32, name=name + "_codes", align_bytes=64)
+            scales = sb.tile([P, S], U8, name=name + "_scales", align_bytes=64)
+            nc.vector.quantize_mx(out=codes[:].bitcast(FP8X4), scales=scales[:], in_=woven[:].rearrange("p j t -> p (j t)"))
+            return codes, scales
+
+        xs = zeroed_bytes(T, "xs")
+        w1s = zeroed_bytes(S, "w1s")
+        ds = zeroed_bytes(G, "ds")
+        ds_placed = zeroed_bytes(S, "ds_placed")
+        offs_t = load_list(offs, "offs_t")
+        load_scale_rows(nc.sync, xs, x_scales)
+        xw = sb.tile([P, T], I32, name="xw")
+        nc.sync.dma_start(xw[:], words_of(x_words))
+        w1w = sb.tile([P, S], I32, name="w1w")
+        nc.sync.dma_start(w1w[:], words_of(w1_words))
+        load_scale_rows(nc.sync, w1s, w1_scales)
+        cand_t = load_list(cand, "cand_t")
+        n3_t = load_list(n3, "n3_t")
+        k1_t = load_list(k1, "k1_t")
+        for r in range(2):
+            nc.sync.dma_start(ds[r:P:16, :].bitcast(I32), d_scales[0, r:16:2, :].bitcast(I32))
+        dw = sb.tile([P, G], I32, name="dw")
+        nc.sync.dma_start(dw[:], words_of(d_words))
+        n2_t = load_list(n2, "n2_t")
+        n4_t = load_list(n4, "n4_t")
+        n1_t = load_list(n1, "n1_t")
+        gs_t = sb.tile([P, PACK], F32, name="gs_t")
+        nc.sync.dma_start(gs_t[:], gs.rearrange("(p t) o -> p (t o)", t=PACK))
+        gk_t = sb.tile([P, PACK], F32, name="gk_t")
+        nc.sync.dma_start(gk_t[:], gk.rearrange("(p t) o -> p (t o)", t=PACK))
+        n5_t = load_list(n5, "n5_t")
+        n6_t = load_list(n6, "n6_t")
+
+        xq_s = gather_bytes(xs, offs_t, "xq_s")
+        xq_w = gather_words(xw, offs_t, "xq_w")
+        w1_w = deal_words(w1w, "w1_w")
+        w1_s = deal_bytes(w1s, "w1_s")
+        y, y3 = [], []
+        for t in planes:
+            bank = psum.tile([P, S], F32, name=f"bank_y{t}", tag=f"low{t}")
+            product(bank, t, w1_w, w1_s, xq_w, xq_s)
+            y_t = sb.tile([P, 2 * S], F32, name=f"y_plane{t}")
+            nc.vector.tensor_copy(y_t[:, :S], bank[:])
+            y3_t = sb.tile([P, S], F32, name=f"y3_{t}", tag=f"y3_{t}", align_bytes=64)
+            nc.scalar.activation(y3_t[:], y_t[:].indirect(n3_t[:]), ACT.Copy)
+            y.append(y_t)
+            y3.append(y3_t)
+
+        st = sb.tile([P, PACK, S], F32, name="st")
+        mag = sb.tile([P, PACK, S], F32, name="mag", tag="mag_then_fetched")
+        logm = []
+        for step in range(PACK + 1):
+            if step < PACK:
+                nc.vector.tensor_tensor(st[:, step, :], y[step][:, :S], y3[step][:], ALU.subtract)
+            if step > 0:
+                t = step - 1
+                nc.vector.scalar_tensor_tensor(mag[:, t, :], st[:, t, :], -1.0, st[:, t, :], ALU.mult, ALU.max)
+                log_t = sb.tile([P, 2 * S], F32, name=f"logm{t}")
+                nc.scalar.activation(log_t[:, :S], mag[:, t, :], ACT.Ln, bias=TINY, scale=2.0)
+                logm.append(log_t)
+
+        key_s_picked = gather_bytes(ds, k1_t, "key_s_picked", "y3_1")
+        for r in range(4):
+            nc.sync.dma_start(ds_placed[r:P:32, :].bitcast(I32), key_s_picked[16 * (r // 2) + r % 2 : P : 32, :].bitcast(I32))
+        cand_s_picked = gather_bytes(xs, cand_t, "cand_s_picked", "y3_2")
+        for r in range(4):
+            nc.sync.dma_start(ds_placed[4 + r : P : 32, :].bitcast(I32), cand_s_picked[r:P:32, :].bitcast(I32))
+        cand_w_picked = gather_words(xw, cand_t, "cand_w_picked", "y3_3")
+
+        gk2 = sb.tile([P, PACK], F32, name="gk2")
+        nc.gpsimd.tensor_scalar(gk2[:], gk_t[:], 2.0, 0.0, ALU.mult, ALU.add)
+
+        fetched = sb.tile([P, 3, PACK, S], F32, name="fetched", tag="mag_then_fetched")
+        sig1, y2, sig4 = fetched[:, 0], fetched[:, 1], fetched[:, 2]
+        larger = sb.tile([P, PACK, S], F32, name="larger")
+        z = sb.tile([P, PACK, S], F32, name="z")
+        z2 = sb.tile([P, PACK, S], F32, name="z2")
+
+        def weigh(t):
+            nc.vector.tensor_scalar(z[:, t, :], larger[:, t, :], gs_t[:, t : t + 1], None, ALU.mult)
+
+        def divide(t):
+            nc.scalar.activation(sig4[:, t, :], logm[t][:].indirect(n4_t[:]), ACT.Sigmoid, scale=-1.0)
+            nc.vector.scalar_tensor_tensor(z2[:, t, :], sig4[:, t, :], gk2[:, t : t + 1], st[:, t, :], ALU.mult, ALU.mult)
+
+        for t in planes:
+            nc.scalar.activation(sig1[:, t, :], y[t][:].indirect(n1_t[:]), ACT.Sigmoid)
+            nc.scalar.activation(y2[:, t, :], y[t][:].indirect(n2_t[:]), ACT.Copy)
+            gated = sb.tile([P, S], F32, name=f"gated{t}", tag=f"gated{t}", align_bytes=64)
+            nc.vector.tensor_tensor(gated[:], y[t][:, :S], sig1[:, t, :], ALU.mult)
+            if t == 0:
+                cand_w = deal_words(cand_w_picked, "cand_w")
+            else:
+                weigh(t - 1)
+            nc.vector.tensor_tensor(larger[:, t, :], gated[:], y2[:, t, :], ALU.max)
+            if t == 0:
+                key_w_picked = gather_words(dw, k1_t, "key_w_picked", "gated0")
+            if t == 1:
+                picked_s = deal_bytes(ds_placed, "picked_s")
+            if t == 2:
+                key_w = deal_words(key_w_picked, "key_w")
+        weigh(PACK - 1)
+        z_woven = weave(z, "zq")
+        divide(0)
+        z_w, z_s = quantise(z_woven, "zq")
+        for t in range(1, PACK):
+            divide(t)
+        z2_w, z2_s = quantise(weave(z2, "z2q"), "z2q")
+
+        a, a5 = [], []
+        for t in planes:
+            bank = psum.tile([P, S], F32, name=f"bank_a{t}", tag=f"high{t}")
+            product(bank, t, cand_w, picked_s, z_w, z_s, 4)
+            a_t = sb.tile([P, S], F32, name=f"a_plane{t}")
+            nc.scalar.activation(a_t[:], bank[:], ACT.Copy, scale=0.0625)
+            a5_t = sb.tile([P, W], F32, name=f"a5_{t}")
+            nc.scalar.activation(a5_t[:], a_t[:].indirect(n5_t[:]), ACT.Copy, scale=-0.5)
+            a.append(a_t)
+            a5.append(a5_t)
+
+        b6 = []
+        for t in planes:
+            bank = psum.tile([P, S], F32, name=f"bank_b{t}", tag=f"low{t}")
+            product(bank, t, key_w, picked_s, z2_w, z2_s)
+            b_t = sb.tile([P, S], F32, name=f"b_plane{t}")
+            b6_t = sb.tile([P, W], F32, name=f"b6_{t}")
+            if t == 0:
+                nc.vector.tensor_scalar(b_t[:], bank[:], 0.0625, None, ALU.mult)
+                nc.vector.tensor_copy(b6_t[:], b_t[:].indirect(n6_t[:]))
+            else:
+                nc.scalar.activation(b_t[:], bank[:], ACT.Copy, scale=0.0625)
+                nc.scalar.activation(b6_t[:], b_t[:].indirect(n6_t[:]), ACT.Copy)
+            b6.append(b6_t)
+
+        out_rows = out_0.rearrange("(p t) j -> p t j", t=PACK)
+        rounded = sb.tile([P, PACK, S], BF16, name="rounded")
+        for t in planes:
+            nc.vector.tensor_tensor(a[t][:].indirect(n5_t[:]), b6[t][:], a5[t][:], ALU.add)
+            nc.sync.dma_start(out_rows[:, t, :], a[t][:])
+            if t < PACK - 1:
+                nc.scalar.copy(rounded[:, t, :], a[t][:])
+            else:
+                nc.vector.tensor_copy(rounded[:, t, :], a[t][:])
+        out_w, out_s = quantise(weave(rounded, "outq", 160), "outq")
+        nc.sync.dma_start(words_of(out_1), out_w[:])
+        for q in range(4):
+            queue = nc.scalar if q % 2 else nc.sync
+            queue.dma_start(out_2[0, 4 * q : 4 * q + 4, :].bitcast(I32), out_s[32 * q : 32 * q + 4, :].bitcast(I32))

@@ -20,6 +20,16 @@ T = 1024
 G = 2048
 FLOPS = 3 * 2 * 512 * 512 * 512
 TINY = 2.0**-60
+EVS = 2
+WS = ()
+ZS = 0
+CUT = 256
+Z2S = 128
+G2V = (0, 1)
+ABS_S = (3,)
+A5V = 3
+B0V = False
+OUTS = 160
 
 
 def tile_picked_cdkeyputbgmaxhopn_none_po_kernel(
@@ -27,6 +37,8 @@ def tile_picked_cdkeyputbgmaxhopn_none_po_kernel(
 ):
     nc = tc.nc
     planes = range(PACK)
+    every = slice(0, S)
+    halves = (slice(0, W), slice(W, S))
 
     def words_of(packed):
         return packed[0].rearrange("p n r -> p (n r)").bitcast(I32)
@@ -42,8 +54,8 @@ def tile_picked_cdkeyputbgmaxhopn_none_po_kernel(
             return tile
 
         def zeroed_bytes(width, name):
-            tile = sb.tile([P, width], U8, name=name, align_bytes=64)
-            nc.vector.memset(tile[:].bitcast(I32), 0)
+            tile = sb.tile([P, width], U8, name=name, tag=name, align_bytes=64)
+            nc.gpsimd.memset(tile[:].bitcast(I32), 0)
             return tile
 
         def load_scale_rows(queue, tile, dram):
@@ -76,42 +88,42 @@ def tile_picked_cdkeyputbgmaxhopn_none_po_kernel(
             nc.vector.tensor_copy(picked[:], table[:].indirect(offsets[:]))
             return picked
 
-        def product(bank, t, lhs_words, lhs_scales, rhs_words, rhs_scales, first_row=0):
+        def product(bank, t, lhs_words, lhs_scales, rhs_words, rhs_scales, first_row=0, places=slice(0, S)):
             cols = slice(P * t, P * (t + 1))
             nc.tensor.matmul_mx(
-                out=bank[:],
+                out=bank[:, places],
                 lhsT=lhs_words[:, cols].bitcast(FP8X4),
                 lhsT_scale=lhs_scales[first_row:, cols],
-                rhs=rhs_words[:].bitcast(FP8X4),
-                rhs_scale=rhs_scales[:],
+                rhs=rhs_words[:, places].bitcast(FP8X4),
+                rhs_scale=rhs_scales[:, places],
                 start=True,
                 stop=True,
             )
 
-        def weave(stacked, name, scalar_cols=0):
-            woven = sb.tile([P, S, PACK], BF16, name=name + "_woven", align_bytes=64)
-            split = S - scalar_cols
-            nc.vector.tensor_copy(
-                woven[:, :split, :].rearrange("p (c i) t -> p c t i", i=4),
-                stacked[:, :, :split].rearrange("p t (c i) -> p c t i", i=4),
+        def weave(engine_copy, woven, stacked, places):
+            engine_copy(
+                woven[:, places, :].rearrange("p (c i) t -> p c t i", i=4),
+                stacked[:, :, places].rearrange("p t (c i) -> p c t i", i=4),
             )
-            if scalar_cols:
-                nc.scalar.copy(
-                    woven[:, split:, :].rearrange("p (c i) t -> p c t i", i=4),
-                    stacked[:, :, split:].rearrange("p t (c i) -> p c t i", i=4),
-                )
-            return woven
 
-        def quantise(woven, name):
+        def mx_tiles(name):
+            woven = sb.tile([P, S, PACK], BF16, name=name + "_woven", tag=name + "_woven", align_bytes=64)
             codes = sb.tile([P, S], I32, name=name + "_codes", align_bytes=64)
             scales = sb.tile([P, S], U8, name=name + "_scales", align_bytes=64)
-            nc.vector.quantize_mx(out=codes[:].bitcast(FP8X4), scales=scales[:], in_=woven[:].rearrange("p j t -> p (j t)"))
-            return codes, scales
+            return woven, codes, scales
+
+        def quantise(woven, codes, scales, places):
+            nc.vector.quantize_mx(
+                out=codes[:, places].bitcast(FP8X4), scales=scales[:, places], in_=woven[:, places, :].rearrange("p j t -> p (j t)")
+            )
 
         xs = zeroed_bytes(T, "xs")
         w1s = zeroed_bytes(S, "w1s")
         ds = zeroed_bytes(G, "ds")
         ds_placed = zeroed_bytes(S, "ds_placed")
+        warm = sb.tile([P, 2], F32, name="warm")
+        nc.gpsimd.memset(warm[:, 0:1], 1.0)
+        nc.scalar.activation(warm[:, 1:2], warm[:, 0:1], ACT.Ln)
         offs_t = load_list(offs, "offs_t")
         load_scale_rows(nc.sync, xs, x_scales)
         xw = sb.tile([P, T], I32, name="xw")
@@ -145,11 +157,19 @@ def tile_picked_cdkeyputbgmaxhopn_none_po_kernel(
             bank = psum.tile([P, S], F32, name=f"bank_y{t}", tag=f"low{t}")
             product(bank, t, w1_w, w1_s, xq_w, xq_s)
             y_t = sb.tile([P, 2 * S], F32, name=f"y_plane{t}")
-            nc.vector.tensor_copy(y_t[:, :S], bank[:])
+            if t < EVS:
+                nc.scalar.copy(y_t[:, :S], bank[:])
+            else:
+                nc.vector.tensor_copy(y_t[:, :S], bank[:])
             y3_t = sb.tile([P, S], F32, name=f"y3_{t}", tag=f"y3_{t}", align_bytes=64)
             nc.scalar.activation(y3_t[:], y_t[:].indirect(n3_t[:]), ACT.Copy)
             y.append(y_t)
             y3.append(y3_t)
+
+        cand_s_picked = gather_bytes(xs, cand_t, "cand_s_picked")
+        cand_w = deal_words(gather_words(xw, cand_t, "cand_w_picked"), "cand_w")
+        for r in range(4):
+            nc.sync.dma_start(ds_placed[4 + r : P : 32, :].bitcast(I32), cand_s_picked[r:P:32, :].bitcast(I32))
 
         st = sb.tile([P, PACK, S], F32, name="st")
         mag = sb.tile([P, PACK, S], F32, name="mag", tag="mag_then_fetched")
@@ -159,30 +179,39 @@ def tile_picked_cdkeyputbgmaxhopn_none_po_kernel(
                 nc.vector.tensor_tensor(st[:, step, :], y[step][:, :S], y3[step][:], ALU.subtract)
             if step > 0:
                 t = step - 1
-                nc.vector.scalar_tensor_tensor(mag[:, t, :], st[:, t, :], -1.0, st[:, t, :], ALU.mult, ALU.max)
+                if t in ABS_S:
+                    nc.scalar.activation(mag[:, t, :], st[:, t, :], ACT.Abs)
+                else:
+                    nc.vector.scalar_tensor_tensor(mag[:, t, :], st[:, t, :], -1.0, st[:, t, :], ALU.mult, ALU.max)
                 log_t = sb.tile([P, 2 * S], F32, name=f"logm{t}")
                 nc.scalar.activation(log_t[:, :S], mag[:, t, :], ACT.Ln, bias=TINY, scale=2.0)
                 logm.append(log_t)
-
         key_s_picked = gather_bytes(ds, k1_t, "key_s_picked", "y3_1")
         for r in range(4):
             nc.sync.dma_start(ds_placed[r:P:32, :].bitcast(I32), key_s_picked[16 * (r // 2) + r % 2 : P : 32, :].bitcast(I32))
-        cand_s_picked = gather_bytes(xs, cand_t, "cand_s_picked", "y3_2")
-        for r in range(4):
-            nc.sync.dma_start(ds_placed[4 + r : P : 32, :].bitcast(I32), cand_s_picked[r:P:32, :].bitcast(I32))
-        cand_w_picked = gather_words(xw, cand_t, "cand_w_picked", "y3_3")
+        key_w_picked = gather_words(dw, k1_t, "key_w_picked", "y3_2")
+        key_w = deal_words(key_w_picked, "key_w")
+        y2v = {}
+        y2_early = sb.tile([P, PACK, S], F32, name="y2_early", tag="y3_3", align_bytes=64)
+        for t in G2V:
+            nc.vector.tensor_copy(y2_early[:, t, :], y[t][:].indirect(n2_t[:]))
+            y2v[t] = y2_early[:, t, :]
+        picked_s = deal_bytes(ds_placed, "picked_s")
+
 
         gk2 = sb.tile([P, PACK], F32, name="gk2")
         nc.gpsimd.tensor_scalar(gk2[:], gk_t[:], 2.0, 0.0, ALU.mult, ALU.add)
 
         fetched = sb.tile([P, 3, PACK, S], F32, name="fetched", tag="mag_then_fetched")
         sig1, y2, sig4 = fetched[:, 0], fetched[:, 1], fetched[:, 2]
-        larger = sb.tile([P, PACK, S], F32, name="larger")
-        z = sb.tile([P, PACK, S], F32, name="z")
-        z2 = sb.tile([P, PACK, S], F32, name="z2")
+        larger = sb.tile([P, PACK, S], F32, name="larger", tag="larger")
+        z = sb.tile([P, PACK, S], F32, name="z", tag="ds_placed", align_bytes=64)
 
         def weigh(t):
-            nc.vector.tensor_scalar(z[:, t, :], larger[:, t, :], gs_t[:, t : t + 1], None, ALU.mult)
+            if t in WS:
+                nc.scalar.activation(z[:, t, :], larger[:, t, :], ACT.Copy, scale=gs_t[:, t : t + 1])
+            else:
+                nc.vector.tensor_scalar(z[:, t, :], larger[:, t, :], gs_t[:, t : t + 1], None, ALU.mult)
 
         def divide(t):
             nc.scalar.activation(sig4[:, t, :], logm[t][:].indirect(n4_t[:]), ACT.Sigmoid, scale=-1.0)
@@ -190,64 +219,78 @@ def tile_picked_cdkeyputbgmaxhopn_none_po_kernel(
 
         for t in planes:
             nc.scalar.activation(sig1[:, t, :], y[t][:].indirect(n1_t[:]), ACT.Sigmoid)
-            nc.scalar.activation(y2[:, t, :], y[t][:].indirect(n2_t[:]), ACT.Copy)
+            if t not in G2V:
+                nc.scalar.activation(y2[:, t, :], y[t][:].indirect(n2_t[:]), ACT.Copy)
             gated = sb.tile([P, S], F32, name=f"gated{t}", tag=f"gated{t}", align_bytes=64)
             nc.vector.tensor_tensor(gated[:], y[t][:, :S], sig1[:, t, :], ALU.mult)
-            if t == 0:
-                cand_w = deal_words(cand_w_picked, "cand_w")
-            else:
+            if t > 0:
                 weigh(t - 1)
-            nc.vector.tensor_tensor(larger[:, t, :], gated[:], y2[:, t, :], ALU.max)
-            if t == 0:
-                key_w_picked = gather_words(dw, k1_t, "key_w_picked", "gated0")
-            if t == 1:
-                picked_s = deal_bytes(ds_placed, "picked_s")
-            if t == 2:
-                key_w = deal_words(key_w_picked, "key_w")
+            nc.vector.tensor_tensor(larger[:, t, :], gated[:], y2v.get(t, y2[:, t, :]), ALU.max)
         weigh(PACK - 1)
-        z_woven = weave(z, "zq")
+        z_woven, z_w, z_s = mx_tiles("zq")
+        z2 = sb.tile([P, PACK, S], F32, name="z2", tag="larger")
+        z2_woven, z2_w, z2_s = mx_tiles("z2q")
         divide(0)
-        z_w, z_s = quantise(z_woven, "zq")
-        for t in range(1, PACK):
+        weave(nc.vector.tensor_copy, z_woven, z, every)
+        divide(1)
+        quantise(z_woven, z_w, z_s, every)
+        for t in range(2, PACK):
             divide(t)
-        z2_w, z2_s = quantise(weave(z2, "z2q"), "z2q")
+        parts = (slice(0, CUT), slice(CUT, S))
+        weave(nc.vector.tensor_copy, z2_woven, z2, parts[0])
+        weave(nc.vector.tensor_copy, z2_woven, z2, slice(CUT, S - Z2S))
+        weave(nc.scalar.copy, z2_woven, z2, slice(S - Z2S, S))
+        for places in parts:
+            quantise(z2_woven, z2_w, z2_s, places)
 
-        a, a5 = [], []
+        a = []
         for t in planes:
             bank = psum.tile([P, S], F32, name=f"bank_a{t}", tag=f"high{t}")
             product(bank, t, cand_w, picked_s, z_w, z_s, 4)
             a_t = sb.tile([P, S], F32, name=f"a_plane{t}")
             nc.scalar.activation(a_t[:], bank[:], ACT.Copy, scale=0.0625)
-            a5_t = sb.tile([P, W], F32, name=f"a5_{t}")
-            nc.scalar.activation(a5_t[:], a_t[:].indirect(n5_t[:]), ACT.Copy, scale=-0.5)
             a.append(a_t)
-            a5.append(a5_t)
+        a5v = sb.tile([P, PACK, W], F32, name="a5v", tag="z2q_woven", align_bytes=64)
+        a5 = []
+        for t in range(A5V):
+            nc.vector.tensor_scalar(a5v[:, t, :], a[t][:].indirect(n5_t[:]), -0.5, 0.0, ALU.mult, ALU.add)
+            a5.append(a5v[:, t, :])
 
         b6 = []
         for t in planes:
             bank = psum.tile([P, S], F32, name=f"bank_b{t}", tag=f"low{t}")
-            product(bank, t, key_w, picked_s, z2_w, z2_s)
-            b_t = sb.tile([P, S], F32, name=f"b_plane{t}")
+            b_t = sb.tile([P, S], F32, name=f"b_plane{t}", tag=f"b_plane{max(t - 1, 0)}")
             b6_t = sb.tile([P, W], F32, name=f"b6_{t}")
             if t == 0:
-                nc.vector.tensor_scalar(b_t[:], bank[:], 0.0625, None, ALU.mult)
-                nc.vector.tensor_copy(b6_t[:], b_t[:].indirect(n6_t[:]))
+                other = psum.tile([P, S], F32, name="bank_b0_rest", tag="high0")
+                for places, part_bank in zip(parts, (bank, other)):
+                    product(part_bank, t, key_w, picked_s, z2_w, z2_s, 0, places)
+                    nc.scalar.activation(b_t[:, places], part_bank[:, places], ACT.Copy, scale=0.0625)
             else:
+                product(bank, t, key_w, picked_s, z2_w, z2_s)
                 nc.scalar.activation(b_t[:], bank[:], ACT.Copy, scale=0.0625)
-                nc.scalar.activation(b6_t[:], b_t[:].indirect(n6_t[:]), ACT.Copy)
+            nc.scalar.activation(b6_t[:], b_t[:].indirect(n6_t[:]), ACT.Copy)
             b6.append(b6_t)
+        a5_last = sb.tile([P, W], F32, name="a5_last", tag="b_plane0")
+        nc.scalar.activation(a5_last[:], a[A5V][:].indirect(n5_t[:]), ACT.Copy, scale=-0.5)
+        a5.append(a5_last[:])
 
         out_rows = out_0.rearrange("(p t) j -> p t j", t=PACK)
         rounded = sb.tile([P, PACK, S], BF16, name="rounded")
         for t in planes:
-            nc.vector.tensor_tensor(a[t][:].indirect(n5_t[:]), b6[t][:], a5[t][:], ALU.add)
+            nc.vector.tensor_tensor(a[t][:].indirect(n5_t[:]), b6[t][:], a5[t], ALU.add)
             nc.sync.dma_start(out_rows[:, t, :], a[t][:])
             if t < PACK - 1:
                 nc.scalar.copy(rounded[:, t, :], a[t][:])
             else:
                 nc.vector.tensor_copy(rounded[:, t, :], a[t][:])
-        out_w, out_s = quantise(weave(rounded, "outq", 160), "outq")
-        nc.sync.dma_start(words_of(out_1), out_w[:])
+        out_woven, out_w, out_s = mx_tiles("outq")
+        weave(nc.vector.tensor_copy, out_woven, rounded, halves[0])
+        weave(nc.vector.tensor_copy, out_woven, rounded, slice(W, S - OUTS))
+        weave(nc.scalar.copy, out_woven, rounded, slice(S - OUTS, S))
+        for places in halves:
+            quantise(out_woven, out_w, out_s, places)
+            nc.sync.dma_start(words_of(out_1)[:, places], out_w[:, places])
         for q in range(4):
             queue = nc.scalar if q % 2 else nc.sync
             queue.dma_start(out_2[0, 4 * q : 4 * q + 4, :].bitcast(I32), out_s[32 * q : 32 * q + 4, :].bitcast(I32))

@@ -20,13 +20,25 @@ T = 1024
 G = 2048
 FLOPS = 3 * 2 * 512 * 512 * 512
 TINY = 2.0**-60
-EVS = 2
+DUPV = ()
+ORDER = (2,0,3,1)
+G2E = ()
+PT = 3
+STT = {3: "y_again0"}
+CWT = "mag3"
+KDT = None
+KWT = "mag0"
+EARLY = {}
+MB = 4
+YT = "y_again1"
+FUSE = (0, 1)
+KST = None
 WS = ()
 ZS = 0
 CUT = 256
 Z2S = 128
-G2V = (0, 1)
-ABS_S = (3,)
+G2V = (0,1,2)
+ABS_S = (0,2,3)
 A5V = 3
 B0V = False
 OUTS = 160
@@ -53,8 +65,8 @@ def tile_picked_cdkeyputbgmaxhopn_none_po_kernel(
             nc.sync.dma_start(tile[:], dram)
             return tile
 
-        def zeroed_bytes(width, name):
-            tile = sb.tile([P, width], U8, name=name, tag=name, align_bytes=64)
+        def zeroed_bytes(width, name, tag=None):
+            tile = sb.tile([P, width], U8, name=name, tag=tag or name, align_bytes=64)
             nc.gpsimd.memset(tile[:].bitcast(I32), 0)
             return tile
 
@@ -62,16 +74,16 @@ def tile_picked_cdkeyputbgmaxhopn_none_po_kernel(
             for q in range(4):
                 queue.dma_start(tile[32 * q : 32 * q + 4, :].bitcast(I32), dram[0, 4 * q : 4 * q + 4, :].bitcast(I32))
 
-        def deal_words(src, name):
-            dealt = sb.tile([P, S], I32, name=name, align_bytes=64)
+        def deal_words(src, name, tag=None):
+            dealt = sb.tile([P, S], I32, name=name, tag=tag or name, align_bytes=64)
             nc.vector.tensor_copy(
                 dealt[:].rearrange("p (t c i) -> p c t i", t=PACK, i=4),
                 src[:].rearrange("p (c i t) -> p c t i", t=PACK, i=4),
             )
             return dealt
 
-        def deal_bytes(src, name):
-            dealt = sb.tile([P, S], U8, name=name, align_bytes=64)
+        def deal_bytes(src, name, tag=None):
+            dealt = sb.tile([P, S], U8, name=name, tag=tag or name, align_bytes=64)
             nc.vector.tensor_copy(
                 dealt[:].rearrange("p (t m) -> p t m", t=PACK),
                 src[:].rearrange("p (m t) -> p t m", t=PACK),
@@ -120,7 +132,6 @@ def tile_picked_cdkeyputbgmaxhopn_none_po_kernel(
         xs = zeroed_bytes(T, "xs")
         w1s = zeroed_bytes(S, "w1s")
         ds = zeroed_bytes(G, "ds")
-        ds_placed = zeroed_bytes(S, "ds_placed")
         warm = sb.tile([P, 2], F32, name="warm")
         nc.gpsimd.memset(warm[:, 0:1], 1.0)
         nc.scalar.activation(warm[:, 1:2], warm[:, 0:1], ACT.Ln)
@@ -128,16 +139,14 @@ def tile_picked_cdkeyputbgmaxhopn_none_po_kernel(
         load_scale_rows(nc.sync, xs, x_scales)
         xw = sb.tile([P, T], I32, name="xw")
         nc.sync.dma_start(xw[:], words_of(x_words))
-        w1w = sb.tile([P, S], I32, name="w1w")
+        w1w = sb.tile([P, S], I32, name="w1w", tag="w1w", align_bytes=64)
         nc.sync.dma_start(w1w[:], words_of(w1_words))
         load_scale_rows(nc.sync, w1s, w1_scales)
-        cand_t = load_list(cand, "cand_t")
         n3_t = load_list(n3, "n3_t")
         k1_t = load_list(k1, "k1_t")
+        cand_t = load_list(cand, "cand_t")
         for r in range(2):
             nc.sync.dma_start(ds[r:P:16, :].bitcast(I32), d_scales[0, r:16:2, :].bitcast(I32))
-        dw = sb.tile([P, G], I32, name="dw")
-        nc.sync.dma_start(dw[:], words_of(d_words))
         n2_t = load_list(n2, "n2_t")
         n4_t = load_list(n4, "n4_t")
         n1_t = load_list(n1, "n1_t")
@@ -149,63 +158,89 @@ def tile_picked_cdkeyputbgmaxhopn_none_po_kernel(
         n6_t = load_list(n6, "n6_t")
 
         xq_s = gather_bytes(xs, offs_t, "xq_s")
-        xq_w = gather_words(xw, offs_t, "xq_w")
-        w1_w = deal_words(w1w, "w1_w")
-        w1_s = deal_bytes(w1s, "w1_s")
-        y, y3 = [], []
-        for t in planes:
-            bank = psum.tile([P, S], F32, name=f"bank_y{t}", tag=f"low{t}")
-            product(bank, t, w1_w, w1_s, xq_w, xq_s)
-            y_t = sb.tile([P, 2 * S], F32, name=f"y_plane{t}")
-            if t < EVS:
-                nc.scalar.copy(y_t[:, :S], bank[:])
+        y = [sb.tile([P, 2 * S], F32, name=f"y_plane{t}") for t in planes]
+        y_again = [sb.tile([P, S], F32, name=f"y_again{t}", tag=f"y_again{t}", align_bytes=64) for t in planes]
+        for half, places in enumerate(halves):
+            entries = slice(16 * half, 16 * (half + 1))
+            xq_w = sb.tile([P, S], I32, name=f"xq_w{half}", tag=("xq_w", "w1s")[half], align_bytes=64)
+            nc.vector.tensor_copy(xq_w[:, places].bitcast(U32), xw[:].bitcast(U32).indirect(offs_t[:, entries]))
+            if half == 0:
+                w1_w = deal_words(w1w, "w1_w")
+                w1_s = deal_bytes(w1s, "w1_s")
+            for t in planes:
+                bank = psum.tile([P, S], F32, name=f"bank_y{half}{t}", tag=("low", "high")[half] + str(t))
+                product(bank, t, w1_w, w1_s, xq_w, xq_s, 0, places)
+                nc.scalar.copy(y[t][:, places], bank[:, places])
+                if half == 1 and t in FUSE and t not in DUPV:
+                    nc.sync.dma_start(y_again[t][:], y[t][:, :S])
+        y2 = {}
+
+        def fetch_y2(t, tag, on_vector):
+            y2_t = sb.tile([P, S], F32, name=f"y2_{t}", tag=tag, align_bytes=64)
+            if on_vector:
+                nc.vector.tensor_copy(y2_t[:], y[t][:].indirect(n2_t[:]))
             else:
-                nc.vector.tensor_copy(y_t[:, :S], bank[:])
-            y3_t = sb.tile([P, S], F32, name=f"y3_{t}", tag=f"y3_{t}", align_bytes=64)
-            nc.scalar.activation(y3_t[:], y_t[:].indirect(n3_t[:]), ACT.Copy)
-            y.append(y_t)
-            y3.append(y3_t)
+                nc.scalar.activation(y2_t[:], y[t][:].indirect(n2_t[:]), ACT.Copy)
+            y2[t] = y2_t[:]
 
         cand_s_picked = gather_bytes(xs, cand_t, "cand_s_picked")
-        cand_w = deal_words(gather_words(xw, cand_t, "cand_w_picked"), "cand_w")
+        cand_w_picked = gather_words(xw, cand_t, "cand_w_picked")
+        for t in DUPV:
+            nc.vector.tensor_copy(y_again[t][:], y[t][:, :S])
+        for t in ORDER:
+            if t not in FUSE:
+                nc.scalar.activation(y_again[t][:], y[t][:].indirect(n3_t[:]), ACT.Copy)
+        for t in G2E:
+            fetch_y2(t, "xq_w_late", False)
+
+        st = {}
+        logm = {}
+        mags = {}
+
+        def log_of(t):
+            log_t = sb.tile([P, 2 * S], F32, name=f"logm{t}")
+            nc.scalar.activation(log_t[:, :S], mags[t][:], ACT.Ln, bias=TINY, scale=2.0)
+            logm[t] = log_t
+
+        for step, t in enumerate(ORDER):
+            st[t] = sb.tile([P, S], F32, name=f"st{t}", tag=STT.get(t, f"st{t}"), align_bytes=64)
+            if t in FUSE:
+                nc.vector.tensor_tensor(st[t][:], y[t][:].indirect(n3_t[:]), y_again[t][:], ALU.subtract)
+            else:
+                nc.vector.tensor_tensor(st[t][:], y_again[t][:], y[t][:, :S], ALU.subtract)
+            mag_t = sb.tile([P, S], F32, name=f"mag{t}", tag=f"mag{(step + 2) % MB}", align_bytes=64)
+            if t in ABS_S:
+                nc.scalar.activation(mag_t[:], st[t][:], ACT.Abs)
+            else:
+                nc.vector.scalar_tensor_tensor(mag_t[:], st[t][:], -1.0, st[t][:], ALU.mult, ALU.max)
+            mags[t] = mag_t
+            if step > 0:
+                log_of(ORDER[step - 1])
+        log_of(ORDER[-1])
+        last = f"y_again{ORDER[-1]}"
+        key_s_picked = gather_bytes(ds, k1_t, "key_s_picked", KST)
+        cand_w = deal_words(cand_w_picked, "cand_w", CWT)
+        dw = sb.tile([P, G], I32, name="dw", tag=f"y_again{ORDER[0]}", align_bytes=64)
+        nc.sync.dma_start(dw[:], words_of(d_words))
+        ds_placed = zeroed_bytes(S, "ds_placed", "mag2")
         for r in range(4):
             nc.sync.dma_start(ds_placed[4 + r : P : 32, :].bitcast(I32), cand_s_picked[r:P:32, :].bitcast(I32))
-
-        st = sb.tile([P, PACK, S], F32, name="st")
-        mag = sb.tile([P, PACK, S], F32, name="mag", tag="mag_then_fetched")
-        logm = []
-        for step in range(PACK + 1):
-            if step < PACK:
-                nc.vector.tensor_tensor(st[:, step, :], y[step][:, :S], y3[step][:], ALU.subtract)
-            if step > 0:
-                t = step - 1
-                if t in ABS_S:
-                    nc.scalar.activation(mag[:, t, :], st[:, t, :], ACT.Abs)
-                else:
-                    nc.vector.scalar_tensor_tensor(mag[:, t, :], st[:, t, :], -1.0, st[:, t, :], ALU.mult, ALU.max)
-                log_t = sb.tile([P, 2 * S], F32, name=f"logm{t}")
-                nc.scalar.activation(log_t[:, :S], mag[:, t, :], ACT.Ln, bias=TINY, scale=2.0)
-                logm.append(log_t)
-        key_s_picked = gather_bytes(ds, k1_t, "key_s_picked", "y3_1")
+        key_w_picked = gather_words(dw, k1_t, "key_w_picked", KWT)
+        key_w = deal_words(key_w_picked, "key_w", KDT)
         for r in range(4):
             nc.sync.dma_start(ds_placed[r:P:32, :].bitcast(I32), key_s_picked[16 * (r // 2) + r % 2 : P : 32, :].bitcast(I32))
-        key_w_picked = gather_words(dw, k1_t, "key_w_picked", "y3_2")
-        key_w = deal_words(key_w_picked, "key_w")
-        y2v = {}
-        y2_early = sb.tile([P, PACK, S], F32, name="y2_early", tag="y3_3", align_bytes=64)
+        y2_mid = sb.tile([P, PACK, S], F32, name="y2_mid", tag=YT, align_bytes=64)
         for t in G2V:
-            nc.vector.tensor_copy(y2_early[:, t, :], y[t][:].indirect(n2_t[:]))
-            y2v[t] = y2_early[:, t, :]
-        picked_s = deal_bytes(ds_placed, "picked_s")
-
+            nc.vector.tensor_copy(y2_mid[:, t, :], y[t][:].indirect(n2_t[:]))
+            y2[t] = y2_mid[:, t, :]
 
         gk2 = sb.tile([P, PACK], F32, name="gk2")
-        nc.gpsimd.tensor_scalar(gk2[:], gk_t[:], 2.0, 0.0, ALU.mult, ALU.add)
+        nc.gpsimd.tensor_scalar(gk2[:], gk_t[:], -2.0, 0.0, ALU.mult, ALU.add)
 
-        fetched = sb.tile([P, 3, PACK, S], F32, name="fetched", tag="mag_then_fetched")
-        sig1, y2, sig4 = fetched[:, 0], fetched[:, 1], fetched[:, 2]
+        fetched = sb.tile([P, 3, PACK, S], F32, name="fetched", tag="mag1", align_bytes=64)
+        sig1, sig4, y2_late = fetched[:, 0], fetched[:, 1], fetched[:, 2]
         larger = sb.tile([P, PACK, S], F32, name="larger", tag="larger")
-        z = sb.tile([P, PACK, S], F32, name="z", tag="ds_placed", align_bytes=64)
+        z = sb.tile([P, PACK, S], F32, name="z", align_bytes=64)
 
         def weigh(t):
             if t in WS:
@@ -215,26 +250,28 @@ def tile_picked_cdkeyputbgmaxhopn_none_po_kernel(
 
         def divide(t):
             nc.scalar.activation(sig4[:, t, :], logm[t][:].indirect(n4_t[:]), ACT.Sigmoid, scale=-1.0)
-            nc.vector.scalar_tensor_tensor(z2[:, t, :], sig4[:, t, :], gk2[:, t : t + 1], st[:, t, :], ALU.mult, ALU.mult)
+            nc.vector.scalar_tensor_tensor(z2[:, t, :], sig4[:, t, :], gk2[:, t : t + 1], st[t][:], ALU.mult, ALU.mult)
 
         for t in planes:
             nc.scalar.activation(sig1[:, t, :], y[t][:].indirect(n1_t[:]), ACT.Sigmoid)
-            if t not in G2V:
-                nc.scalar.activation(y2[:, t, :], y[t][:].indirect(n2_t[:]), ACT.Copy)
+            for u in (t, EARLY.get(t, t)):
+                if u not in y2:
+                    nc.scalar.activation(y2_late[:, u, :], y[u][:].indirect(n2_t[:]), ACT.Copy)
+                    y2[u] = y2_late[:, u, :]
             gated = sb.tile([P, S], F32, name=f"gated{t}", tag=f"gated{t}", align_bytes=64)
             nc.vector.tensor_tensor(gated[:], y[t][:, :S], sig1[:, t, :], ALU.mult)
             if t > 0:
                 weigh(t - 1)
-            nc.vector.tensor_tensor(larger[:, t, :], gated[:], y2v.get(t, y2[:, t, :]), ALU.max)
+            nc.vector.tensor_tensor(larger[:, t, :], gated[:], y2[t], ALU.max)
         weigh(PACK - 1)
+        picked_s = deal_bytes(ds_placed, "picked_s", "gated3")
         z_woven, z_w, z_s = mx_tiles("zq")
         z2 = sb.tile([P, PACK, S], F32, name="z2", tag="larger")
         z2_woven, z2_w, z2_s = mx_tiles("z2q")
-        divide(0)
         weave(nc.vector.tensor_copy, z_woven, z, every)
-        divide(1)
+        divide(0)
         quantise(z_woven, z_w, z_s, every)
-        for t in range(2, PACK):
+        for t in range(1, PACK):
             divide(t)
         parts = (slice(0, CUT), slice(CUT, S))
         weave(nc.vector.tensor_copy, z2_woven, z2, parts[0])
@@ -258,9 +295,9 @@ def tile_picked_cdkeyputbgmaxhopn_none_po_kernel(
 
         b6 = []
         for t in planes:
-            bank = psum.tile([P, S], F32, name=f"bank_b{t}", tag=f"low{t}")
-            b_t = sb.tile([P, S], F32, name=f"b_plane{t}", tag=f"b_plane{max(t - 1, 0)}")
-            b6_t = sb.tile([P, W], F32, name=f"b6_{t}")
+            bank = psum.tile([P, S], F32, name=f"bank_b{t}", tag="high0" if t == 2 else "low0")
+            b_t = sb.tile([P, S], F32, name=f"b_plane{t}", tag=f"b_plane{t}")
+            b6_t = sb.tile([P, W], F32, name=f"b6_{t}", tag=f"b6_{t}")
             if t == 0:
                 other = psum.tile([P, S], F32, name="bank_b0_rest", tag="high0")
                 for places, part_bank in zip(parts, (bank, other)):
@@ -271,12 +308,13 @@ def tile_picked_cdkeyputbgmaxhopn_none_po_kernel(
                 nc.scalar.activation(b_t[:], bank[:], ACT.Copy, scale=0.0625)
             nc.scalar.activation(b6_t[:], b_t[:].indirect(n6_t[:]), ACT.Copy)
             b6.append(b6_t)
-        a5_last = sb.tile([P, W], F32, name="a5_last", tag="b_plane0")
+
+        a5_last = sb.tile([P, W], F32, name="a5_last", tag="b_plane1")
         nc.scalar.activation(a5_last[:], a[A5V][:].indirect(n5_t[:]), ACT.Copy, scale=-0.5)
         a5.append(a5_last[:])
 
         out_rows = out_0.rearrange("(p t) j -> p t j", t=PACK)
-        rounded = sb.tile([P, PACK, S], BF16, name="rounded")
+        rounded = sb.tile([P, PACK, S], BF16, name="rounded", tag="b_plane3")
         for t in planes:
             nc.vector.tensor_tensor(a[t][:].indirect(n5_t[:]), b6[t][:], a5[t], ALU.add)
             nc.sync.dma_start(out_rows[:, t, :], a[t][:])

@@ -23,7 +23,8 @@ TINY = 2.0**-60
 DUPV = ()
 ORDER = (2,0,3,1)
 G2E = ()
-PT = 3
+A3 = -1
+AV = (3,)
 STT = {3: "y_again0"}
 CWT = "mag3"
 KDT = None
@@ -39,7 +40,7 @@ CUT = 256
 Z2S = 128
 G2V = (0,1,2)
 ABS_S = (0,2,3)
-A5V = 3
+A5V = 2
 B0V = False
 OUTS = 160
 
@@ -118,8 +119,8 @@ def tile_picked_cdkeyputbgmaxhopn_none_po_kernel(
                 stacked[:, :, places].rearrange("p t (c i) -> p c t i", i=4),
             )
 
-        def mx_tiles(name):
-            woven = sb.tile([P, S, PACK], BF16, name=name + "_woven", tag=name + "_woven", align_bytes=64)
+        def mx_tiles(name, tag=None):
+            woven = sb.tile([P, S, PACK], BF16, name=name + "_woven", tag=tag or name + "_woven", align_bytes=64)
             codes = sb.tile([P, S], I32, name=name + "_codes", align_bytes=64)
             scales = sb.tile([P, S], U8, name=name + "_scales", align_bytes=64)
             return woven, codes, scales
@@ -236,11 +237,15 @@ def tile_picked_cdkeyputbgmaxhopn_none_po_kernel(
 
         gk2 = sb.tile([P, PACK], F32, name="gk2")
         nc.gpsimd.tensor_scalar(gk2[:], gk_t[:], -2.0, 0.0, ALU.mult, ALU.add)
+        stk = sb.tile([P, PACK, S], F32, name="stk", tag="cand_w_picked", align_bytes=64)
+        for t in planes:
+            nc.gpsimd.tensor_scalar(stk[:, t, :], st[t][:], gk2[:, t : t + 1], 0.0, ALU.mult, ALU.add)
 
         fetched = sb.tile([P, 3, PACK, S], F32, name="fetched", tag="mag1", align_bytes=64)
-        sig1, sig4, y2_late = fetched[:, 0], fetched[:, 1], fetched[:, 2]
-        larger = sb.tile([P, PACK, S], F32, name="larger", tag="larger")
-        z = sb.tile([P, PACK, S], F32, name="z", align_bytes=64)
+        sig1, y2_late = fetched[:, 0], fetched[:, 2]
+        sig4 = fetched[:, 1].rearrange("p (h a) (b w) -> p h (a b) w", h=2, b=2)
+        larger = sb.tile([P, PACK, S], F32, name="larger", tag="larger", align_bytes=64)
+        z = sb.tile([P, PACK, S], F32, name="z", tag="z", align_bytes=64)
 
         def weigh(t):
             if t in WS:
@@ -248,9 +253,16 @@ def tile_picked_cdkeyputbgmaxhopn_none_po_kernel(
             else:
                 nc.vector.tensor_scalar(z[:, t, :], larger[:, t, :], gs_t[:, t : t + 1], None, ALU.mult)
 
-        def divide(t):
-            nc.scalar.activation(sig4[:, t, :], logm[t][:].indirect(n4_t[:]), ACT.Sigmoid, scale=-1.0)
-            nc.vector.scalar_tensor_tensor(z2[:, t, :], sig4[:, t, :], gk2[:, t : t + 1], st[t][:], ALU.mult, ALU.mult)
+        def divide(half):
+            places = halves[half]
+            for t in planes:
+                nc.scalar.activation(sig4[:, half, t, :], logm[t][:].indirect(n4_t[:, 16 * half : 16 * (half + 1)]), ACT.Sigmoid, scale=-1.0)
+            nc.vector.tensor_tensor(
+                z2_woven[:, places, :].rearrange("p (c i) t -> p c t i", i=4),
+                sig4[:, half].rearrange("p t (c i) -> p c t i", i=4),
+                stk[:, :, places].rearrange("p t (c i) -> p c t i", i=4),
+                ALU.mult,
+            )
 
         for t in planes:
             nc.scalar.activation(sig1[:, t, :], y[t][:].indirect(n1_t[:]), ACT.Sigmoid)
@@ -266,29 +278,31 @@ def tile_picked_cdkeyputbgmaxhopn_none_po_kernel(
         weigh(PACK - 1)
         picked_s = deal_bytes(ds_placed, "picked_s", "gated3")
         z_woven, z_w, z_s = mx_tiles("zq")
-        z2 = sb.tile([P, PACK, S], F32, name="z2", tag="larger")
-        z2_woven, z2_w, z2_s = mx_tiles("z2q")
         weave(nc.vector.tensor_copy, z_woven, z, every)
-        divide(0)
         quantise(z_woven, z_w, z_s, every)
-        for t in range(1, PACK):
-            divide(t)
-        parts = (slice(0, CUT), slice(CUT, S))
-        weave(nc.vector.tensor_copy, z2_woven, z2, parts[0])
-        weave(nc.vector.tensor_copy, z2_woven, z2, slice(CUT, S - Z2S))
-        weave(nc.scalar.copy, z2_woven, z2, slice(S - Z2S, S))
-        for places in parts:
-            quantise(z2_woven, z2_w, z2_s, places)
+        z2_woven, z2_w, z2_s = mx_tiles("z2q", "zq_woven")
+        divide(0)
+        divide(1)
+        quantise(z2_woven, z2_w, z2_s, halves[0])
+        quantise(z2_woven, z2_w, z2_s, halves[1])
+        parts = halves
 
         a = []
-        for t in planes:
+
+        def score(t, tag):
             bank = psum.tile([P, S], F32, name=f"bank_a{t}", tag=f"high{t}")
             product(bank, t, cand_w, picked_s, z_w, z_s, 4)
-            a_t = sb.tile([P, S], F32, name=f"a_plane{t}")
-            nc.scalar.activation(a_t[:], bank[:], ACT.Copy, scale=0.0625)
+            a_t = sb.tile([P, S], F32, name=f"a_plane{t}", tag=tag, align_bytes=64)
+            if t in AV:
+                nc.vector.tensor_scalar(a_t[:], bank[:], 0.0625, None, ALU.mult)
+            else:
+                nc.scalar.activation(a_t[:], bank[:], ACT.Copy, scale=0.0625)
             a.append(a_t)
-        a5v = sb.tile([P, PACK, W], F32, name="a5v", tag="z2q_woven", align_bytes=64)
+
+        for t in range(A5V if A3 >= 0 else PACK):
+            score(t, "zq_woven" if t in AV else f"a_plane{t}")
         a5 = []
+        a5v = sb.tile([P, PACK, W], F32, name="a5v", tag="cand_w_picked", align_bytes=64)
         for t in range(A5V):
             nc.vector.tensor_scalar(a5v[:, t, :], a[t][:].indirect(n5_t[:]), -0.5, 0.0, ALU.mult, ALU.add)
             a5.append(a5v[:, t, :])
@@ -296,7 +310,7 @@ def tile_picked_cdkeyputbgmaxhopn_none_po_kernel(
         b6 = []
         for t in planes:
             bank = psum.tile([P, S], F32, name=f"bank_b{t}", tag="high0" if t == 2 else "low0")
-            b_t = sb.tile([P, S], F32, name=f"b_plane{t}", tag=f"b_plane{t}")
+            b_t = sb.tile([P, S], F32, name=f"b_plane{t}", tag=f"b_plane{t}", align_bytes=64)
             b6_t = sb.tile([P, W], F32, name=f"b6_{t}", tag=f"b6_{t}")
             if t == 0:
                 other = psum.tile([P, S], F32, name="bank_b0_rest", tag="high0")
@@ -308,13 +322,16 @@ def tile_picked_cdkeyputbgmaxhopn_none_po_kernel(
                 nc.scalar.activation(b_t[:], bank[:], ACT.Copy, scale=0.0625)
             nc.scalar.activation(b6_t[:], b_t[:].indirect(n6_t[:]), ACT.Copy)
             b6.append(b6_t)
+            if t == A3:
+                score(PACK - 1, f"b_plane{t}")
+            if t >= A5V:
+                a5_t = sb.tile([P, W], F32, name=f"a5_{t}", tag=f"b_plane{t - 1}" if A5V < 3 else "b_plane1", align_bytes=64)
+                nc.scalar.activation(a5_t[:], a[t][:].indirect(n5_t[:]), ACT.Copy, scale=-0.5)
+                a5.append(a5_t[:])
 
-        a5_last = sb.tile([P, W], F32, name="a5_last", tag="b_plane1")
-        nc.scalar.activation(a5_last[:], a[A5V][:].indirect(n5_t[:]), ACT.Copy, scale=-0.5)
-        a5.append(a5_last[:])
 
         out_rows = out_0.rearrange("(p t) j -> p t j", t=PACK)
-        rounded = sb.tile([P, PACK, S], BF16, name="rounded", tag="b_plane3")
+        rounded = sb.tile([P, PACK, S], BF16, name="rounded", tag="b_plane3", align_bytes=64)
         for t in planes:
             nc.vector.tensor_tensor(a[t][:].indirect(n5_t[:]), b6[t][:], a5[t], ALU.add)
             nc.sync.dma_start(out_rows[:, t, :], a[t][:])

from contextlib import ExitStack

import concourse.mybir as mybir

F32 = mybir.dt.float32
BF16 = mybir.dt.bfloat16
I32 = mybir.dt.int32
U32 = mybir.dt.uint32
U16 = mybir.dt.uint16
U8 = mybir.dt.uint8
FP8X4 = mybir.dt.float8_e4m3fn_x4
ALU = mybir.AluOpType
ACT = mybir.ActivationFunctionType

P = 128
PACK = 4
S = 512
W = 256
T = 1024
G = 2048
FLOPS = 3 * 2 * 512 * 512 * 512
TINY = 2.0**-60
DUPV = ()
ORDER = (2,0,3,1)
G2E = ()
A3 = -1
AV = (3,)
STT = {3: "y_again0"}
CWT = "mag3"
KDT = None
KWT = "mag0"
EARLY = {}
MB = 4
YT = "y_again1"
FUSE = (0, 1)
KST = None
WS = ()
ZS = 0
CUT = 256
Z2S = 128
G2V = (0,1,2)
ABS_S = (0,2,3)
A5V = 2
B0V = False
OUTS = 160


def tile_picked_cdkeyputbgmaxhopn_none_po_kernel(
    tc, x_words, x_scales, w1_words, w1_scales, gs, gk, d_words, d_scales, offs, n1, n2, n3, n4, cand, k1, n5, n6, out_0, out_1, out_2
):
    nc = tc.nc
    planes = range(PACK)
    every = slice(0, S)
    halves = (slice(0, W), slice(W, S))

    def words_of(packed):
        return packed[0].rearrange("p n r -> p (n r)").bitcast(I32)

    with ExitStack() as ctx:
        lists = ctx.enter_context(tc.tile_pool(name="lists", bufs=1))
        sb = ctx.enter_context(tc.tile_pool(name="sb", bufs=1))
        psum = ctx.enter_context(tc.psum_pool(name="psum", bufs=1))

        def load_list(dram, name):
            tile = lists.tile([P, dram.shape[1]], U16, name=name)
            nc.sync.dma_start(tile[:], dram)
            return tile

        def zeroed_bytes(width, name, tag=None):
            tile = sb.tile([P, width], U8, name=name, tag=tag or name, align_bytes=64)
            nc.gpsimd.memset(tile[:].bitcast(I32), 0)
            return tile

        def load_scale_rows(queue, tile, dram):
            for q in range(4):
                queue.dma_start(tile[32 * q : 32 * q + 4, :].bitcast(I32), dram[0, 4 * q : 4 * q + 4, :].bitcast(I32))

        def deal_words(src, name, tag=None):
            dealt = sb.tile([P, S], I32, name=name, tag=tag or name, align_bytes=64)
            nc.vector.tensor_copy(
                dealt[:].rearrange("p (t c i) -> p c t i", t=PACK, i=4),
                src[:].rearrange("p (c i t) -> p c t i", t=PACK, i=4),
            )
            return dealt

        def deal_bytes(src, name, tag=None):
            dealt = sb.tile([P, S], U8, name=name, tag=tag or name, align_bytes=64)
            nc.vector.tensor_copy(
                dealt[:].rearrange("p (t m) -> p t m", t=PACK),
                src[:].rearrange("p (m t) -> p t m", t=PACK),
            )
            return dealt

        def gather_words(table, offsets, name, tag=None):
            picked = sb.tile([P, S], I32, name=name, tag=tag or name, align_bytes=64)
            nc.vector.tensor_copy(picked[:].bitcast(U32), table[:].bitcast(U32).indirect(offsets[:]))
            return picked

        def gather_bytes(table, offsets, name, tag=None):
            picked = sb.tile([P, S], U8, name=name, tag=tag or name, align_bytes=64)
            nc.vector.tensor_copy(picked[:], table[:].indirect(offsets[:]))
            return picked

        def product(bank, t, lhs_words, lhs_scales, rhs_words, rhs_scales, first_row=0, places=slice(0, S)):
            cols = slice(P * t, P * (t + 1))
            nc.tensor.matmul_mx(
                out=bank[:, places],
                lhsT=lhs_words[:, cols].bitcast(FP8X4),
                lhsT_scale=lhs_scales[first_row:, cols],
                rhs=rhs_words[:, places].bitcast(FP8X4),
                rhs_scale=rhs_scales[:, places],
                start=True,
                stop=True,
            )

        def weave(engine_copy, woven, stacked, places):
            engine_copy(
                woven[:, places, :].rearrange("p (c i) t -> p c t i", i=4),
                stacked[:, :, places].rearrange("p t (c i) -> p c t i", i=4),
            )

        def mx_tiles(name, tag=None):
            woven = sb.tile([P, S, PACK], BF16, name=name + "_woven", tag=tag or name + "_woven", align_bytes=64)
            codes = sb.tile([P, S], I32, name=name + "_codes", align_bytes=64)
            scales = sb.tile([P, S], U8, name=name + "_scales", align_bytes=64)
            return woven, codes, scales

        def quantise(woven, codes, scales, places):
            nc.vector.quantize_mx(
                out=codes[:, places].bitcast(FP8X4), scales=scales[:, places], in_=woven[:, places, :].rearrange("p j t -> p (j t)")
            )

        xs = zeroed_bytes(T, "xs")
        w1s = zeroed_bytes(S, "w1s")
        ds = zeroed_bytes(G, "ds")
        warm = sb.tile([P, 2], F32, name="warm")
        nc.gpsimd.memset(warm[:, 0:1], 1.0)
        nc.scalar.activation(warm[:, 1:2], warm[:, 0:1], ACT.Ln)
        offs_t = load_list(offs, "offs_t")
        load_scale_rows(nc.sync, xs, x_scales)
        xw = sb.tile([P, T], I32, name="xw")
        nc.sync.dma_start(xw[:], words_of(x_words))
        w1w = sb.tile([P, S], I32, name="w1w", tag="w1w", align_bytes=64)
        nc.sync.dma_start(w1w[:], words_of(w1_words))
        load_scale_rows(nc.sync, w1s, w1_scales)
        n3_t = load_list(n3, "n3_t")
        k1_t = load_list(k1, "k1_t")
        cand_t = load_list(cand, "cand_t")
        for r in range(2):
            nc.sync.dma_start(ds[r:P:16, :].bitcast(I32), d_scales[0, r:16:2, :].bitcast(I32))
        n2_t = load_list(n2, "n2_t")
        n4_t = load_list(n4, "n4_t")
        n1_t = load_list(n1, "n1_t")
        gs_t = sb.tile([P, PACK], F32, name="gs_t")
        nc.sync.dma_start(gs_t[:], gs.rearrange("(p t) o -> p (t o)", t=PACK))
        gk_t = sb.tile([P, PACK], F32, name="gk_t")
        nc.sync.dma_start(gk_t[:], gk.rearrange("(p t) o -> p (t o)", t=PACK))
        n5_t = load_list(n5, "n5_t")
        n6_t = load_list(n6, "n6_t")

        xq_s = gather_bytes(xs, offs_t, "xq_s")
        y = [sb.tile([P, 2 * S], F32, name=f"y_plane{t}") for t in planes]
        y_again = [sb.tile([P, S], F32, name=f"y_again{t}", tag=f"y_again{t}", align_bytes=64) for t in planes]
        for half, places in enumerate(halves):
            entries = slice(16 * half, 16 * (half + 1))
            xq_w = sb.tile([P, S], I32, name=f"xq_w{half}", tag=("xq_w", "w1s")[half], align_bytes=64)
            nc.vector.tensor_copy(xq_w[:, places].bitcast(U32), xw[:].bitcast(U32).indirect(offs_t[:, entries]))
            if half == 0:
                w1_w = deal_words(w1w, "w1_w")
                w1_s = deal_bytes(w1s, "w1_s")
            for t in planes:
                bank = psum.tile([P, S], F32, name=f"bank_y{half}{t}", tag=("low", "high")[half] + str(t))
                product(bank, t, w1_w, w1_s, xq_w, xq_s, 0, places)
                nc.scalar.copy(y[t][:, places], bank[:, places])
                if half == 1 and t in FUSE and t not in DUPV:
                    nc.sync.dma_start(y_again[t][:], y[t][:, :S])
        y2 = {}

        def fetch_y2(t, tag, on_vector):
            y2_t = sb.tile([P, S], F32, name=f"y2_{t}", tag=tag, align_bytes=64)
            if on_vector:
                nc.vector.tensor_copy(y2_t[:], y[t][:].indirect(n2_t[:]))
            else:
                nc.scalar.activation(y2_t[:], y[t][:].indirect(n2_t[:]), ACT.Copy)
            y2[t] = y2_t[:]

        cand_s_picked = gather_bytes(xs, cand_t, "cand_s_picked")
        cand_w_picked = gather_words(xw, cand_t, "cand_w_picked")
        for t in DUPV:
            nc.vector.tensor_copy(y_again[t][:], y[t][:, :S])
        for t in ORDER:
            if t not in FUSE:
                nc.scalar.activation(y_again[t][:], y[t][:].indirect(n3_t[:]), ACT.Copy)
        for t in G2E:
            fetch_y2(t, "xq_w_late", False)

        st = {}
        logm = {}
        mags = {}

        def log_of(t):
            log_t = sb.tile([P, 2 * S], F32, name=f"logm{t}")
            nc.scalar.activation(log_t[:, :S], mags[t][:], ACT.Ln, bias=TINY, scale=2.0)
            logm[t] = log_t

        for step, t in enumerate(ORDER):
            st[t] = sb.tile([P, S], F32, name=f"st{t}", tag=STT.get(t, f"st{t}"), align_bytes=64)
            if t in FUSE:
                nc.vector.tensor_tensor(st[t][:], y[t][:].indirect(n3_t[:]), y_again[t][:], ALU.subtract)
            else:
                nc.vector.tensor_tensor(st[t][:], y_again[t][:], y[t][:, :S], ALU.subtract)
            mag_t = sb.tile([P, S], F32, name=f"mag{t}", tag=f"mag{(step + 2) % MB}", align_bytes=64)
            if t in ABS_S:
                nc.scalar.activation(mag_t[:], st[t][:], ACT.Abs)
            else:
                nc.vector.scalar_tensor_tensor(mag_t[:], st[t][:], -1.0, st[t][:], ALU.mult, ALU.max)
            mags[t] = mag_t
            if step > 0:
                log_of(ORDER[step - 1])
        log_of(ORDER[-1])
        last = f"y_again{ORDER[-1]}"
        key_s_picked = gather_bytes(ds, k1_t, "key_s_picked", KST)
        cand_w = deal_words(cand_w_picked, "cand_w", CWT)
        dw = sb.tile([P, G], I32, name="dw", tag=f"y_again{ORDER[0]}", align_bytes=64)
        nc.sync.dma_start(dw[:], words_of(d_words))
        ds_placed = zeroed_bytes(S, "ds_placed", "mag2")
        for r in range(4):
            nc.sync.dma_start(ds_placed[4 + r : P : 32, :].bitcast(I32), cand_s_picked[r:P:32, :].bitcast(I32))
        key_w_picked = gather_words(dw, k1_t, "key_w_picked", KWT)
        key_w = deal_words(key_w_picked, "key_w", KDT)
        for r in range(4):
            nc.sync.dma_start(ds_placed[r:P:32, :].bitcast(I32), key_s_picked[16 * (r // 2) + r % 2 : P : 32, :].bitcast(I32))
        y2_mid = sb.tile([P, PACK, S], F32, name="y2_mid", tag=YT, align_bytes=64)
        for t in G2V:
            nc.vector.tensor_copy(y2_mid[:, t, :], y[t][:].indirect(n2_t[:]))
            y2[t] = y2_mid[:, t, :]

        gk2 = sb.tile([P, PACK], F32, name="gk2")
        nc.gpsimd.tensor_scalar(gk2[:], gk_t[:], -2.0, 0.0, ALU.mult, ALU.add)
        stk = sb.tile([P, PACK, S], F32, name="stk", tag="cand_w_picked", align_bytes=64)
        for t in planes:
            nc.gpsimd.tensor_scalar(stk[:, t, :], st[t][:], gk2[:, t : t + 1], 0.0, ALU.mult, ALU.add)

        fetched = sb.tile([P, 3, PACK, S], F32, name="fetched", tag="mag1", align_bytes=64)
        sig1, y2_late = fetched[:, 0], fetched[:, 2]
        sig4 = fetched[:, 1].rearrange("p (h a) (b w) -> p h (a b) w", h=2, b=2)
        larger = sb.tile([P, PACK, S], F32, name="larger", tag="larger", align_bytes=64)
        z = sb.tile([P, PACK, S], F32, name="z", tag="z", align_bytes=64)

        def weigh(t):
            if t in WS:
                nc.scalar.activation(z[:, t, :], larger[:, t, :], ACT.Copy, scale=gs_t[:, t : t + 1])
            else:
                nc.vector.tensor_scalar(z[:, t, :], larger[:, t, :], gs_t[:, t : t + 1], None, ALU.mult)

        def divide(half):
            places = halves[half]
            for t in planes:
                nc.scalar.activation(sig4[:, half, t, :], logm[t][:].indirect(n4_t[:, 16 * half : 16 * (half + 1)]), ACT.Sigmoid, scale=-1.0)
            nc.vector.tensor_tensor(
                z2_woven[:, places, :].rearrange("p (c i) t -> p c t i", i=4),
                sig4[:, half].rearrange("p t (c i) -> p c t i", i=4),
                stk[:, :, places].rearrange("p t (c i) -> p c t i", i=4),
                ALU.mult,
            )

        for t in planes:
            nc.scalar.activation(sig1[:, t, :], y[t][:].indirect(n1_t[:]), ACT.Sigmoid)
            for u in (t, EARLY.get(t, t)):
                if u not in y2:
                    nc.scalar.activation(y2_late[:, u, :], y[u][:].indirect(n2_t[:]), ACT.Copy)
                    y2[u] = y2_late[:, u, :]
            gated = sb.tile([P, S], F32, name=f"gated{t}", tag=f"gated{t}", align_bytes=64)
            nc.vector.tensor_tensor(gated[:], y[t][:, :S], sig1[:, t, :], ALU.mult)
            if t > 0:
                weigh(t - 1)
            nc.vector.tensor_tensor(larger[:, t, :], gated[:], y2[t], ALU.max)
        weigh(PACK - 1)
        picked_s = deal_bytes(ds_placed, "picked_s", "gated3")
        z_woven, z_w, z_s = mx_tiles("zq")
        weave(nc.vector.tensor_copy, z_woven, z, every)
        quantise(z_woven, z_w, z_s, every)
        z2_woven, z2_w, z2_s = mx_tiles("z2q", "zq_woven")
        divide(0)
        divide(1)
        quantise(z2_woven, z2_w, z2_s, halves[0])
        quantise(z2_woven, z2_w, z2_s, halves[1])
        parts = halves

        a = []

        def score(t, tag):
            bank = psum.tile([P, S], F32, name=f"bank_a{t}", tag=f"high{t}")
            product(bank, t, cand_w, picked_s, z_w, z_s, 4)
            a_t = sb.tile([P, S], F32, name=f"a_plane{t}", tag=tag, align_bytes=64)
            if t in AV:
                nc.vector.tensor_scalar(a_t[:], bank[:], 0.0625, None, ALU.mult)
            else:
                nc.scalar.activation(a_t[:], bank[:], ACT.Copy, scale=0.0625)
            a.append(a_t)

        for t in range(A5V if A3 >= 0 else PACK):
            score(t, "zq_woven" if t in AV else f"a_plane{t}")
        a5 = []
        a5v = sb.tile([P, PACK, W], F32, name="a5v", tag="cand_w_picked", align_bytes=64)
        for t in range(A5V):
            nc.vector.tensor_scalar(a5v[:, t, :], a[t][:].indirect(n5_t[:]), -0.5, 0.0, ALU.mult, ALU.add)
            a5.append(a5v[:, t, :])

        b6 = []
        for t in planes:
            bank = psum.tile([P, S], F32, name=f"bank_b{t}", tag="high0" if t == 2 else "low0")
            b_t = sb.tile([P, S], F32, name=f"b_plane{t}", tag=f"b_plane{t}", align_bytes=64)
            b6_t = sb.tile([P, W], F32, name=f"b6_{t}", tag=f"b6_{t}")
            if t == 0:
                other = psum.tile([P, S], F32, name="bank_b0_rest", tag="high0")
                for places, part_bank in zip(parts, (bank, other)):
                    product(part_bank, t, key_w, picked_s, z2_w, z2_s, 0, places)
                    nc.scalar.activation(b_t[:, places], part_bank[:, places], ACT.Copy, scale=0.0625)
            else:
                product(bank, t, key_w, picked_s, z2_w, z2_s)
                nc.scalar.activation(b_t[:], bank[:], ACT.Copy, scale=0.0625)
            nc.scalar.activation(b6_t[:], b_t[:].indirect(n6_t[:]), ACT.Copy)
            b6.append(b6_t)
            if t == A3:
                score(PACK - 1, f"b_plane{t}")
            if t >= A5V:
                a5_t = sb.tile([P, W], F32, name=f"a5_{t}", tag=f"b_plane{t - 1}" if A5V < 3 else "b_plane1", align_bytes=64)
                nc.scalar.activation(a5_t[:], a[t][:].indirect(n5_t[:]), ACT.Copy, scale=-0.5)
                a5.append(a5_t[:])


        out_rows = out_0.rearrange("(p t) j -> p t j", t=PACK)
        rounded = sb.tile([P, PACK, S], BF16, name="rounded", tag="b_plane3", align_bytes=64)
        for t in planes:
            nc.vector.tensor_tensor(a[t][:].indirect(n5_t[:]), b6[t][:], a5[t], ALU.add)
            nc.sync.dma_start(out_rows[:, t, :], a[t][:])
            if t < PACK - 1:
                nc.scalar.copy(rounded[:, t, :], a[t][:])
            else:
                nc.vector.tensor_copy(rounded[:, t, :], a[t][:])
        out_woven, out_w, out_s = mx_tiles("outq")
        weave(nc.vector.tensor_copy, out_woven, rounded, halves[0])
        weave(nc.vector.tensor_copy, out_woven, rounded, slice(W, S - OUTS))
        weave(nc.scalar.copy, out_woven, rounded, slice(S - OUTS, S))
        for places in halves:
            quantise(out_woven, out_w, out_s, places)
            nc.sync.dma_start(words_of(out_1)[:, places], out_w[:, places])
        for q in range(4):
            queue = nc.scalar if q % 2 else nc.sync
            queue.dma_start(out_2[0, 4 * q : 4 * q + 4, :].bitcast(I32), out_s[32 * q : 32 * q + 4, :].bitcast(I32))
